import numpy as np
import ml_dtypes


def mxq(x, axis, fmt="e4m3"):
    dtype, down = {"e4m3": (ml_dtypes.float8_e4m3fn, 7), "e5m2": (ml_dtypes.float8_e5m2, 14)}[fmt]
    v = np.moveaxis(np.asarray(x, np.float32).astype(ml_dtypes.bfloat16).astype(np.float64), axis, -1)
    blocks = v.reshape(v.shape[:-1] + (-1, 32))
    amax = np.abs(blocks).max(-1, keepdims=True)
    byte = np.maximum(np.where(amax > 0, np.frexp(amax)[1] - 1 + 127, 0) - down, 1)
    scale = np.exp2(byte - 127.0)
    codes = (blocks / scale).astype(np.float32).astype(dtype).astype(np.float64)
    return np.moveaxis((codes * scale).reshape(v.shape), -1, axis)


WIDE = False


def mx_kscale(k):
    if not WIDE:
        return np.ones(k)
    levels = np.array([10, -10, 5, -5, 0])
    if k % 512:
        return np.exp2(np.random.permutation(np.resize(levels, k // 32))).repeat(32)
    a = np.empty((k // 512, 16))
    for p in range(k // 512):
        a[p, :8] = np.random.permutation(np.resize(levels, 8))
        for g in range(8):
            far = levels[np.abs(levels - a[p, g]) >= 10]
            a[p, g + 8] = far[np.random.randint(len(far))]
    return np.exp2(a.ravel()).repeat(32)


def f64(x):
    return np.asarray(x).astype(np.float64)


def striped(idx):
    return np.tile(np.asarray(idx).reshape(-1, 16).T, (8, 1)).astype(np.uint16)


def unstriped(offs):
    return offs[:16].T.reshape(-1).astype(np.int64)


E2M1 = np.array([0.0, 0.5, 1.0, 1.5, 2.0, 3.0, 4.0, 6.0, -0.0, -0.5, -1.0, -1.5, -2.0, -3.0, -4.0, -6.0])


def pack_weight(w, fmt):
    k, n = w.shape
    w = f64(np.asarray(w, np.float32).astype(ml_dtypes.bfloat16)).reshape(k // 32, 32, n)
    amax = np.abs(w).max(1)
    if fmt == "e4m3":
        byte = np.frexp(amax)[1] - 1 + 127 - 7
    else:
        mant, ex = np.frexp(amax / 6.0)
        byte = np.where(mant > 0.5, ex, ex - 1) + 127
    byte = np.clip(np.where(amax > 0, byte, 1), 1, 254)
    scaled = (w * np.exp2(127.0 - byte)[:, None, :]).reshape(k, n).astype(np.float32)
    by_word = np.ascontiguousarray(scaled.reshape(k // 512, 128, 4, n).transpose(0, 1, 3, 2))
    if fmt == "e4m3":
        words = by_word.astype(ml_dtypes.float8_e4m3fn).view(np.uint8)
    else:
        c = by_word.astype(ml_dtypes.float4_e2m1fn).view(np.uint8) & 0xF
        words = (c[..., 0::2] | (c[..., 1::2] << 4)).reshape(k // 512, 128, 2 * n)
    return np.ascontiguousarray(words), np.ascontiguousarray(byte.astype(np.uint8).reshape(k // 512, 16, n))


def unpack_weight(words, scales, fmt):
    g, _, n = scales.shape
    words = np.ascontiguousarray(words).reshape(g, 128, n, -1)
    if fmt == "e4m3":
        vals = words.view(ml_dtypes.float8_e4m3fn).astype(np.float64)
    else:
        nib = np.empty((g, 128, n, 4), np.uint8)
        nib[..., 0::2] = words & 0xF
        nib[..., 1::2] = words >> 4
        vals = E2M1[nib]
    vals = vals * np.repeat(np.exp2(scales.astype(np.float64) - 127.0), 8, axis=1)[..., None]
    return vals.transpose(0, 1, 3, 2).reshape(g * 512, n)


def softplus(v):
    return np.log(1.0 + np.exp(v))


D, K, R, T, I, Q, G = 512, 512, 512, 2048, 512, 128, 64


def setup_inputs():
    n = np.random.standard_normal
    idx3 = np.random.permutation(I)[:I]
    idx = np.random.permutation(T)[:I]
    fd = mx_kscale(D)
    fk = mx_kscale(K)
    fr = mx_kscale(R)
    keysp = pack_weight(n((D, T)) / fd[:, None], "e2m1")
    tabp = pack_weight(n((K, T)) / fk[:, None], "e2m1")
    return {
        "query": (n((D, Q)) * 0.6 / np.sqrt(D) * fd[:, None]).astype(np.float32),
        "keys_words": keysp[0],
        "keys_scales": keysp[1],
        "sharp": (np.random.uniform(1.0, 3.0, (Q, 1))).astype(np.float32),
        "tab_words": tabp[0],
        "tab_scales": tabp[1],
        "w1": (n((K, R)) * 1 / np.sqrt(K) * fk[:, None]).astype(np.float32),
        "lam": (np.random.uniform(0.3, 1.0, (R, 1))).astype(np.float32),
        "gout": (n((R, Q)) * 1 / np.sqrt(R) * fr[:, None]).astype(np.float32),
        "hsc": (np.random.uniform(0.7, 1.4, (R, 1)) / fr[:, None]).astype(np.float32),
        "old": (0.5 * n((Q, T))).astype(np.float32),
        "offs3": striped(idx3),
        "offs": striped(idx),
    }


def reference(query, keys_words, keys_scales, sharp, tab_words, tab_scales, w1, lam, gout, hsc, old, offs3, offs):
    idx3 = unstriped(offs3)
    idx = unstriped(offs)
    keysu = unpack_weight(keys_words, keys_scales, "e2m1")
    tabu = unpack_weight(tab_words, tab_scales, "e2m1")
    queryq = mxq(f64(query), 0, "e4m3")
    keysidxg = keysu[:, idx]
    a = queryq.T @ keysidxg
    p = np.exp(a)
    s = p.reshape(Q, G, I // G).sum(axis=2)
    ms = a.reshape(Q, G, I // G).mean(axis=2) * f64(sharp)
    pg = np.exp(ms - np.max(ms, axis=1, keepdims=True))
    z = np.sum(pg, axis=1, keepdims=True)
    sh = pg / z / s
    rr = np.repeat(sh, I // G, axis=1)
    w1q = mxq(f64(w1), 0, "e4m3")
    tabidxg = tabu[:, idx]
    zh = w1q.T @ tabidxg
    ht = softplus(zh)
    hv = ht + ht[:, idx3] * f64(lam)
    hs1 = hv * f64(hsc)
    goutq = mxq(f64(gout), 0, "e4m3")
    hs1q = mxq(hs1, 0, "e4m3")
    c0 = goutq.T @ hs1q
    drr = c0 * p
    dsh = drr.reshape(Q, G, I // G).sum(axis=2)
    dz = np.sum(dsh / s * pg / np.square(z) * (-1.0), axis=1, keepdims=True)
    dpg = dsh / s / z + dz
    dms = dpg * pg
    e1 = dms * f64(sharp) / 8.0
    r1 = np.repeat(e1, I // G, axis=1)
    ds = dsh * pg / z / np.square(s) * (-1.0)
    r2 = np.repeat(ds, I // G, axis=1)
    dp = c0 * rr + r2
    da = r1 + dp * p
    gs = da * 512.0
    gf = np.zeros((Q, T))
    gf[:, idx] = gs
    y = f64(old) + gf
    return y

@@ -1,0 +1,232 @@
+from contextlib import ExitStack
+
+import concourse.mybir as mybir
+
+F32 = mybir.dt.float32
+BF16 = mybir.dt.bfloat16
+I32 = mybir.dt.int32
+U32 = mybir.dt.uint32
+U16 = mybir.dt.uint16
+U8 = mybir.dt.uint8
+FP8X4 = mybir.dt.float8_e4m3fn_x4
+FP4X4 = mybir.dt.float4_e2m1fn_x4
+ALU = mybir.AluOpType
+ACT = mybir.ActivationFunctionType
+AX = mybir.AxisListType
+
+P = 128
+PACK = 4
+T = 2048
+SLOTS = 512
+ROWS = 128
+HIDDEN = 512
+GROUPS = 64
+GSIZE = 8
+WINDOW = SLOTS + 32
+HALF = SLOTS // 2
+CHUNK = 512
+
+FLOPS = 2 * 512 * 128 * 512 * 2 + 2 * 512 * 512 * 512
+
+
+def over_group(ap):
+    return ap.rearrange("p (g o) -> p g o", o=1).to_broadcast([P, GROUPS, GSIZE])
+
+
+def by_group(ap):
+    return ap.rearrange("p (g j) -> p g j", j=GSIZE)
+
+
+def tile_attend_blrlent_bygroup_kernel(tc, query, keys_words, keys_scales, sharp, tab_words, tab_scales,
+                                        w1, lam, gout, hsc, old, offs3, offs, out):
+    nc = tc.nc
+    with ExitStack() as ctx:
+        lists = ctx.enter_context(tc.tile_pool(name="lists", bufs=1))
+        sb = ctx.enter_context(tc.tile_pool(name="sb", bufs=1))
+        psum = ctx.enter_context(tc.psum_pool(name="psum", bufs=1))
+
+        def tile(shape, dtype, name, tag=None):
+            return sb.tile(shape, dtype, name=name, tag=tag or name, align_bytes=64)
+
+        idx = lists.tile([P, SLOTS // 16], U16, name="idx")
+        idx3 = lists.tile([P, SLOTS // 16], U16, name="idx3")
+
+        k_words = tile([P, T], U16, "k_words")
+        k_bytes = tile([P, T], U8, "k_bytes")
+        t_words = tile([P, T], U16, "t_words")
+        t_bytes = tile([P, T], U8, "t_bytes")
+        w_raw = [tile([P, PACK, HIDDEN // 2], F32, "w_raw0")]
+        lam_sb = tile([P, PACK], F32, "lam_sb")
+        hsc_sb = tile([P, PACK], F32, "hsc_sb")
+        placed = tile([P, T], F32, "placed")
+        ht = [tile([P, WINDOW], F32, "ht%d" % t) for t in range(PACK)]
+
+        nc.gpsimd.memset(t_bytes[:].bitcast(I32), 0)
+        nc.vector.memset(k_bytes[:].bitcast(I32), 0)
+        for t in range(PACK):
+            nc.vector.memset(ht[t][:, SLOTS:WINDOW], 0.0)
+        nc.vector.memset(placed[:], 0.0)
+
+        def load_bytes(queue, dst, src):
+            for quad in range(4):
+                queue.dma_start(out=dst[32 * quad:32 * quad + 4, :].bitcast(I32),
+                                in_=src[0, 4 * quad:4 * quad + 4, :].bitcast(I32))
+
+        w_view = w1.rearrange("(p j) c -> p j c", j=PACK)
+        nc.sync.dma_start(idx[:], offs)
+        nc.sync.dma_start(out=lam_sb[:], in_=lam.rearrange("(p t) o -> p (t o)", t=PACK))
+        nc.sync.dma_start(out=hsc_sb[:], in_=hsc.rearrange("(p t) o -> p (t o)", t=PACK))
+        nc.sync.dma_start(out=t_words[:].bitcast(I32), in_=tab_words[0].bitcast(I32))
+        load_bytes(nc.scalar, t_bytes, tab_scales)
+        nc.sync.dma_start(out=w_raw[0][:], in_=w_view[:, :, 0:HIDDEN // 2])
+        nc.sync.dma_start(out=k_words[:].bitcast(I32), in_=keys_words[0].bitcast(I32))
+        load_bytes(nc.gpsimd, k_bytes, keys_scales)
+        nc.sync.dma_start(idx3[:], offs3)
+
+        lh = [tile([P, SLOTS], F32, "lh%d" % t) for t in range(PACK)]
+        for t in range(PACK):
+            nc.vector.tensor_scalar(out=lh[t][:], in0=lam_sb[:, t:t + 1].to_broadcast([P, SLOTS]),
+                                    scalar1=hsc_sb[:, t:t + 1], scalar2=None, op0=ALU.mult)
+
+        tg_words = tile([P, SLOTS], U16, "tg_words")
+        tg_bytes = tile([P, SLOTS], U8, "tg_bytes")
+        nc.vector.tensor_copy(tg_words[:], t_words[:].indirect(idx[:]))
+        nc.vector.tensor_copy(tg_bytes[:], t_bytes[:].indirect(idx[:]))
+        w_raw.append(tile([P, PACK, HIDDEN // 2], F32, "w_raw1", tag="t_words"))
+        nc.sync.dma_start(out=w_raw[1][:], in_=w_view[:, :, HIDDEN // 2:HIDDEN])
+        q_raw = tile([P, PACK, ROWS], F32, "q_raw", tag="t_bytes")
+        nc.sync.dma_start(out=q_raw[:], in_=query.rearrange("(p j) c -> p j c", j=PACK))
+        kg_words = tile([P, SLOTS], U16, "kg_words")
+        kg_bytes = tile([P, SLOTS], U8, "kg_bytes")
+        nc.vector.tensor_copy(kg_words[:], k_words[:].indirect(idx[:]))
+        nc.vector.tensor_copy(kg_bytes[:], k_bytes[:].indirect(idx[:]))
+
+        sharp_sb = tile([P, 1], F32, "sharp_sb", tag="lam_sb")
+        nc.sync.dma_start(out=sharp_sb[:], in_=sharp)
+
+        def interleave(dst, src):
+            nc.scalar.copy(out=dst[:].rearrange("p (c i) j -> p c j i", i=4),
+                           in_=src[:].rearrange("p j (c i) -> p c j i", i=4))
+
+        w_bf = tile([P, PACK, P, PACK], BF16, "w_bf")
+        for h in range(2):
+            nc.scalar.copy(out=w_bf[:, :, 64 * h:64 * (h + 1), :].rearrange("p t m j -> p m j t"),
+                           in_=w_raw[h][:].rearrange("p j (m t) -> p m j t", t=PACK))
+
+        q_bf = tile([P, ROWS, PACK], BF16, "q_bf")
+        q_codes = tile([P, ROWS], U32, "q_codes")
+        q_scales = tile([P, ROWS], U8, "q_scales")
+        interleave(q_bf, q_raw)
+        g_raw = tile([P, PACK, ROWS], F32, "g_raw", tag="k_bytes")
+        nc.sync.dma_start(out=g_raw[:], in_=gout.rearrange("(p j) c -> p j c", j=PACK))
+        old_sb = [tile([P, T // 2], F32, "old%d" % h, tag=("w_raw0", "k_words")[h]) for h in range(2)]
+        for h in range(2):
+            nc.sync.dma_start(out=old_sb[h][:], in_=old[:, h * T // 2:(h + 1) * T // 2])
+
+        sh8 = tile([P, 1], F32, "sh8")
+        nsh8 = tile([P, 1], F32, "nsh8")
+        nc.vector.tensor_scalar(out=sh8[:], in0=sharp_sb[:], scalar1=1.0 / GSIZE, scalar2=None, op0=ALU.mult)
+        nc.vector.tensor_scalar(out=nsh8[:], in0=sharp_sb[:], scalar1=-1.0 / GSIZE, scalar2=None, op0=ALU.mult)
+
+        w_codes = tile([P, PACK, P], U32, "w_codes")
+        w_scales = tile([P, PACK, P], U8, "w_scales")
+        zh_ps = [psum.tile([P, SLOTS], F32, name="zh%d" % t) for t in range(PACK)]
+        ez = [tile([P, SLOTS], F32, "ez%d" % t) for t in range(PACK)]
+        for t in range(PACK):
+            nc.vector.quantize_mx(out=w_codes[:, t, :].bitcast(FP8X4), scales=w_scales[:, t, :],
+                                  in_=w_bf[:, t, :, :].rearrange("p m j -> p (m j)"))
+        nc.vector.quantize_mx(out=q_codes[:].bitcast(FP8X4), scales=q_scales[:],
+                              in_=q_bf[:].rearrange("p c j -> p (c j)"))
+        a_ps = psum.tile([P, SLOTS], F32, name="a_ps")
+        for t in range(PACK):
+            nc.tensor.matmul_mx(out=zh_ps[t][:], lhsT=w_codes[:, t, :].bitcast(FP8X4), lhsT_scale=w_scales[:, t, :],
+                                rhs=tg_words[:].bitcast(FP4X4), rhs_scale=tg_bytes[:], start=True, stop=True)
+            if t == 0:
+                nc.tensor.matmul_mx(out=a_ps[:], lhsT=q_codes[:].bitcast(FP8X4), lhsT_scale=q_scales[:],
+                                    rhs=kg_words[:].bitcast(FP4X4), rhs_scale=kg_bytes[:], start=True, stop=True)
+            nc.scalar.activation(out=ez[t][:], in_=zh_ps[t][:], func=ACT.Exp)
+
+        a_max = tile([P, GROUPS], F32, "a_max")
+        nc.vector.tensor_reduce(out=a_max[:], in_=by_group(a_ps[:]), axis=AX.X, op=ALU.max)
+
+        a_sum = tile([P, GROUPS], F32, "a_sum")
+        a_rel = tile([P, SLOTS], F32, "a_rel")
+        neg_ms = tile([P, GROUPS], F32, "neg_ms")
+        neg_top = tile([P, 1], F32, "neg_top")
+        nc.vector.tensor_reduce(out=a_sum[:], in_=by_group(a_ps[:]), axis=AX.X, op=ALU.add)
+        nc.vector.tensor_tensor(out=by_group(a_rel[:]), in0=by_group(a_ps[:]), in1=over_group(a_max[:]), op=ALU.subtract)
+        nc.vector.tensor_scalar(out=neg_ms[:], in0=a_sum[:], scalar1=nsh8[:], scalar2=None,
+                                op0=ALU.mult, op1=ALU.min, accum_out=neg_top[:])
+        p = tile([P, SLOTS], F32, "p")
+        pg = tile([P, GROUPS], F32, "pg")
+        z = tile([P, 1], F32, "z")
+        nc.scalar.activation(out=p[:], in_=a_rel[:], func=ACT.Exp)
+        nc.scalar.activation(out=pg[:], in_=neg_ms[:], func=ACT.Exp, scale=-1.0, bias=neg_top[:], accum_out=z[:])
+
+        s = tile([P, GROUPS], F32, "s")
+        rs = tile([P, GROUPS], F32, "rs")
+        rz = tile([P, 1], F32, "rz")
+        w512 = tile([P, GROUPS], F32, "w512")
+        nws = tile([P, GROUPS], F32, "nws")
+        pn = tile([P, SLOTS], F32, "pn")
+        weight = tile([P, SLOTS], F32, "weight")
+        nc.vector.tensor_reduce(out=s[:], in_=by_group(p[:]), axis=AX.X, op=ALU.add)
+        nc.vector.reciprocal(out=rz[:], in_=z[:])
+        nc.vector.reciprocal(out=rs[:], in_=s[:])
+        nc.vector.tensor_scalar(out=w512[:], in0=pg[:], scalar1=rz[:], scalar2=512.0, op0=ALU.mult, op1=ALU.mult)
+        nc.vector.tensor_tensor(out=by_group(pn[:]), in0=by_group(p[:]), in1=over_group(rs[:]), op=ALU.mult)
+        nc.vector.tensor_scalar(out=nws[:], in0=pg[:], scalar1=rz[:], scalar2=nsh8[:], op0=ALU.mult, op1=ALU.mult)
+        nc.vector.tensor_tensor(out=by_group(weight[:]), in0=by_group(pn[:]), in1=over_group(w512[:]), op=ALU.mult)
+
+        own = tile([P, PACK, SLOTS], F32, "own")
+        linked = tile([P, PACK, SLOTS], F32, "linked")
+        for t in range(PACK):
+            nc.scalar.activation(out=ht[t][:, 0:SLOTS], in_=ez[t][:], func=ACT.Ln, bias=1.0)
+        for t in range(PACK):
+            nc.vector.tensor_tensor(linked[:, t, :], ht[t][:].indirect(idx3[:]), lh[t][:], ALU.mult)
+            nc.scalar.activation(out=own[:, t, :], in_=ht[t][:, 0:SLOTS], func=ACT.Copy, scale=hsc_sb[:, t:t + 1])
+
+        g_bf = tile([P, ROWS, PACK], BF16, "g_bf")
+        g_codes = tile([P, ROWS], U32, "g_codes")
+        g_scales = tile([P, ROWS], U8, "g_scales")
+        interleave(g_bf, g_raw)
+        spread = tile([P, SLOTS], F32, "spread")
+        nc.scalar.activation(out=spread[:], in_=pn[:], func=ACT.Identity, scale=-1.0, bias=sh8[:])
+
+        h_bf = [tile([P, HALF, PACK], BF16, "h_bf%d" % h) for h in range(2)]
+        h_codes = [tile([P, HALF], U32, "h_codes%d" % h) for h in range(2)]
+        h_scales = [tile([P, HALF], U8, "h_scales%d" % h) for h in range(2)]
+        for h in range(2):
+            cols = slice(h * HALF, (h + 1) * HALF)
+            nc.vector.tensor_tensor(out=h_bf[h][:].rearrange("p (c i) t -> p c t i", i=4),
+                                    in0=own[:, :, cols].rearrange("p t (c i) -> p c t i", i=4),
+                                    in1=linked[:, :, cols].rearrange("p t (c i) -> p c t i", i=4), op=ALU.add)
+        nc.vector.quantize_mx(out=g_codes[:].bitcast(FP8X4), scales=g_scales[:],
+                              in_=g_bf[:].rearrange("p c j -> p (c j)"))
+        c0_ps = psum.tile([P, SLOTS], F32, name="c0_ps")
+        for h in range(2):
+            nc.vector.quantize_mx(out=h_codes[h][:].bitcast(FP8X4), scales=h_scales[h][:],
+                                  in_=h_bf[h][:].rearrange("p c t -> p (c t)"))
+            nc.tensor.matmul_mx(out=c0_ps[:, h * HALF:(h + 1) * HALF], lhsT=g_codes[:].bitcast(FP8X4),
+                                lhsT_scale=g_scales[:], rhs=h_codes[h][:].bitcast(FP8X4), rhs_scale=h_scales[h][:],
+                                start=True, stop=True)
+
+        direct = tile([P, SLOTS], F32, "direct")
+        total = tile([P, 1], F32, "total")
+        v = tile([P, GROUPS], F32, "v")
+        first = tile([P, SLOTS], F32, "first")
+        second = tile([P, SLOTS], F32, "second")
+        nc.vector.scalar_tensor_tensor(out=direct[:], in0=c0_ps[:], scalar=1.0, in1=weight[:],
+                                       op0=ALU.mult, op1=ALU.mult, accum_out=total[:])
+        nc.vector.tensor_reduce(out=v[:], in_=by_group(direct[:]), axis=AX.X, op=ALU.add)
+        nc.vector.scalar_tensor_tensor(out=by_group(first[:]), in0=over_group(nws[:]), scalar=total[:],
+                                       in1=by_group(direct[:]), op0=ALU.mult, op1=ALU.add)
+        nc.vector.tensor_tensor(out=by_group(second[:]), in0=by_group(spread[:]), in1=over_group(v[:]), op=ALU.mult)
+        nc.vector.tensor_tensor(placed[:].indirect(idx[:]), first[:], second[:], ALU.add)
+
+        for c in range(T // CHUNK):
+            cols = slice(c * CHUNK, (c + 1) * CHUNK)
+            part = old_sb[c // 2][:, (c % 2) * CHUNK:(c % 2 + 1) * CHUNK]
+            nc.vector.tensor_tensor(out=part, in0=part, in1=placed[:, cols], op=ALU.add)
+            queue = nc.sync if c % 2 == 0 else nc.scalar
+            queue.dma_start(out=out[:, cols], in_=part)

@@ -30,7 +30,7 @@ FLOPS = 2 * 512 * 128 * 512 * 2 + 2 * 512 * 512 * 512
 
 
 def over_group(ap):
-    return ap.rearrange("p (g o) -> p g o", o=1).to_broadcast([P, GROUPS, GSIZE])
+    return ap.rearrange("p (g o) -> p g o", o=1).to_broadcast([P, ap.shape[1], GSIZE])
 
 
 def by_group(ap):
@@ -51,11 +51,10 @@ def tile_attend_blrlent_bygroup_kernel(tc, query, keys_words, keys_scales, sharp
         idx = lists.tile([P, SLOTS // 16], U16, name="idx")
         idx3 = lists.tile([P, SLOTS // 16], U16, name="idx3")
 
-        k_words = tile([P, T], U16, "k_words")
         k_bytes = tile([P, T], U8, "k_bytes")
         t_words = tile([P, T], U16, "t_words")
         t_bytes = tile([P, T], U8, "t_bytes")
-        w_raw = [tile([P, PACK, HIDDEN // 2], F32, "w_raw0")]
+        w_raw = [tile([P, PACK, HIDDEN // 2], F32, "w_raw%d" % h) for h in range(2)]
         lam_sb = tile([P, PACK], F32, "lam_sb")
         hsc_sb = tile([P, PACK], F32, "hsc_sb")
         placed = tile([P, T], F32, "placed")
@@ -64,11 +63,11 @@ def tile_attend_blrlent_bygroup_kernel(tc, query, keys_words, keys_scales, sharp
         nc.gpsimd.memset(t_bytes[:].bitcast(I32), 0)
         nc.vector.memset(k_bytes[:].bitcast(I32), 0)
         for t in range(PACK):
-            nc.vector.memset(ht[t][:, SLOTS:WINDOW], 0.0)
+            nc.gpsimd.memset(ht[t][:, SLOTS:WINDOW], 0.0)
         nc.vector.memset(placed[:], 0.0)
 
-        def load_bytes(queue, dst, src):
-            for quad in range(4):
+        def load_bytes(queues, dst, src):
+            for quad, queue in enumerate(queues):
                 queue.dma_start(out=dst[32 * quad:32 * quad + 4, :].bitcast(I32),
                                 in_=src[0, 4 * quad:4 * quad + 4, :].bitcast(I32))
 
@@ -76,112 +75,92 @@ def tile_attend_blrlent_bygroup_kernel(tc, query, keys_words, keys_scales, sharp
         nc.sync.dma_start(idx[:], offs)
         nc.sync.dma_start(out=lam_sb[:], in_=lam.rearrange("(p t) o -> p (t o)", t=PACK))
         nc.sync.dma_start(out=hsc_sb[:], in_=hsc.rearrange("(p t) o -> p (t o)", t=PACK))
-        nc.sync.dma_start(out=t_words[:].bitcast(I32), in_=tab_words[0].bitcast(I32))
-        load_bytes(nc.scalar, t_bytes, tab_scales)
-        nc.sync.dma_start(out=w_raw[0][:], in_=w_view[:, :, 0:HIDDEN // 2])
-        nc.sync.dma_start(out=k_words[:].bitcast(I32), in_=keys_words[0].bitcast(I32))
-        load_bytes(nc.gpsimd, k_bytes, keys_scales)
         nc.sync.dma_start(idx3[:], offs3)
+        nc.sync.dma_start(out=t_words[:].bitcast(I32), in_=tab_words[0].bitcast(I32))
+        load_bytes([nc.scalar] * 4, t_bytes, tab_scales)
+        nc.sync.dma_start(out=w_raw[0][:], in_=w_view[:, :, 0:HIDDEN // 2])
+        nc.sync.dma_start(out=w_raw[1][:], in_=w_view[:, :, HIDDEN // 2:HIDDEN])
+        load_bytes([nc.sync, nc.gpsimd, nc.gpsimd, nc.gpsimd], k_bytes, keys_scales)
 
         lh = [tile([P, SLOTS], F32, "lh%d" % t) for t in range(PACK)]
         for t in range(PACK):
             nc.vector.tensor_scalar(out=lh[t][:], in0=lam_sb[:, t:t + 1].to_broadcast([P, SLOTS]),
                                     scalar1=hsc_sb[:, t:t + 1], scalar2=None, op0=ALU.mult)
 
+        k_words = tile([P, T], U16, "k_words", tag="lam_sb")
+        nc.sync.dma_start(out=k_words[:].bitcast(I32), in_=keys_words[0].bitcast(I32))
+
         tg_words = tile([P, SLOTS], U16, "tg_words")
         tg_bytes = tile([P, SLOTS], U8, "tg_bytes")
         nc.vector.tensor_copy(tg_words[:], t_words[:].indirect(idx[:]))
         nc.vector.tensor_copy(tg_bytes[:], t_bytes[:].indirect(idx[:]))
-        w_raw.append(tile([P, PACK, HIDDEN // 2], F32, "w_raw1", tag="t_words"))
-        nc.sync.dma_start(out=w_raw[1][:], in_=w_view[:, :, HIDDEN // 2:HIDDEN])
-        q_raw = tile([P, PACK, ROWS], F32, "q_raw", tag="t_bytes")
-        nc.sync.dma_start(out=q_raw[:], in_=query.rearrange("(p j) c -> p j c", j=PACK))
-        kg_words = tile([P, SLOTS], U16, "kg_words")
-        kg_bytes = tile([P, SLOTS], U8, "kg_bytes")
-        nc.vector.tensor_copy(kg_words[:], k_words[:].indirect(idx[:]))
-        nc.vector.tensor_copy(kg_bytes[:], k_bytes[:].indirect(idx[:]))
+        q_and_sharp = tile([P, PACK * ROWS + 8], F32, "q_and_sharp", tag="t_words")
+        q_raw = q_and_sharp[:, 0:PACK * ROWS].rearrange("p (j c) -> p j c", j=PACK)
+        sharp_sb = q_and_sharp[:, PACK * ROWS:PACK * ROWS + 1]
+        nc.sync.dma_start(out=q_raw, in_=query.rearrange("(p j) c -> p j c", j=PACK))
+        nc.sync.dma_start(out=sharp_sb, in_=sharp)
 
-        sharp_sb = tile([P, 1], F32, "sharp_sb", tag="lam_sb")
-        nc.sync.dma_start(out=sharp_sb[:], in_=sharp)
-
-        def interleave(dst, src):
-            nc.scalar.copy(out=dst[:].rearrange("p (c i) j -> p c j i", i=4),
-                           in_=src[:].rearrange("p j (c i) -> p c j i", i=4))
+        def interleave(copy, dst, src):
+            copy(out=dst[:].rearrange("p (c i) j -> p c j i", i=4), in_=src.rearrange("p j (c i) -> p c j i", i=4))
 
         w_bf = tile([P, PACK, P, PACK], BF16, "w_bf")
-        for h in range(2):
-            nc.scalar.copy(out=w_bf[:, :, 64 * h:64 * (h + 1), :].rearrange("p t m j -> p m j t"),
-                           in_=w_raw[h][:].rearrange("p j (m t) -> p m j t", t=PACK))
+        for copy, h, m0, m1 in ((nc.scalar.copy, 0, 0, 64), (nc.scalar.copy, 1, 0, 24), (nc.vector.tensor_copy, 1, 24, 64)):
+            copy(out=w_bf[:, :, 64 * h + m0:64 * h + m1, :].rearrange("p t m j -> p m j t"),
+                 in_=w_raw[h][:, :, PACK * m0:PACK * m1].rearrange("p j (m t) -> p m j t", t=PACK))
 
-        q_bf = tile([P, ROWS, PACK], BF16, "q_bf")
-        q_codes = tile([P, ROWS], U32, "q_codes")
-        q_scales = tile([P, ROWS], U8, "q_scales")
-        interleave(q_bf, q_raw)
-        g_raw = tile([P, PACK, ROWS], F32, "g_raw", tag="k_bytes")
-        nc.sync.dma_start(out=g_raw[:], in_=gout.rearrange("(p j) c -> p j c", j=PACK))
-        old_sb = [tile([P, T // 2], F32, "old%d" % h, tag=("w_raw0", "k_words")[h]) for h in range(2)]
-        for h in range(2):
-            nc.sync.dma_start(out=old_sb[h][:], in_=old[:, h * T // 2:(h + 1) * T // 2])
-
-        sh8 = tile([P, 1], F32, "sh8")
-        nsh8 = tile([P, 1], F32, "nsh8")
-        nc.vector.tensor_scalar(out=sh8[:], in0=sharp_sb[:], scalar1=1.0 / GSIZE, scalar2=None, op0=ALU.mult)
-        nc.vector.tensor_scalar(out=nsh8[:], in0=sharp_sb[:], scalar1=-1.0 / GSIZE, scalar2=None, op0=ALU.mult)
-
-        w_codes = tile([P, PACK, P], U32, "w_codes")
-        w_scales = tile([P, PACK, P], U8, "w_scales")
+        zero = tile([P, 1], F32, "zero")
+        nc.gpsimd.memset(zero[:], 0.0)
+        w_codes = [tile([P, P], U32, "w_codes%d" % t) for t in range(PACK)]
+        w_scales = [tile([P, P], U8, "w_scales%d" % t) for t in range(PACK)]
         zh_ps = [psum.tile([P, SLOTS], F32, name="zh%d" % t) for t in range(PACK)]
         ez = [tile([P, SLOTS], F32, "ez%d" % t) for t in range(PACK)]
         for t in range(PACK):
-            nc.vector.quantize_mx(out=w_codes[:, t, :].bitcast(FP8X4), scales=w_scales[:, t, :],
+            nc.vector.quantize_mx(out=w_codes[t][:].bitcast(FP8X4), scales=w_scales[t][:],
                                   in_=w_bf[:, t, :, :].rearrange("p m j -> p (m j)"))
+            nc.tensor.matmul_mx(out=zh_ps[t][:], lhsT=w_codes[t][:].bitcast(FP8X4), lhsT_scale=w_scales[t][:],
+                                rhs=tg_words[:].bitcast(FP4X4), rhs_scale=tg_bytes[:], start=True, stop=True)
+            nc.scalar.activation(out=ez[t][:], in_=zh_ps[t][:], func=ACT.Exp, bias=zero[:])
+
+        kg_words = tile([P, SLOTS], U16, "kg_words", tag="w_bf")
+        kg_bytes = tile([P, SLOTS], U8, "kg_bytes", tag="w_scales0")
+        nc.vector.tensor_copy(kg_words[:], k_words[:].indirect(idx[:]))
+        nc.vector.tensor_copy(kg_bytes[:], k_bytes[:].indirect(idx[:]))
+        q_bf = tile([P, ROWS, PACK], BF16, "q_bf", tag="w_codes0")
+        q_codes = tile([P, ROWS], U32, "q_codes")
+        q_scales = tile([P, ROWS], U8, "q_scales")
+        interleave(nc.vector.tensor_copy, q_bf, q_raw)
+        sh8 = tile([P, 1], F32, "sh8")
+        nsh8 = tile([P, 1], F32, "nsh8")
+        nc.vector.tensor_scalar(out=sh8[:], in0=sharp_sb, scalar1=1.0 / GSIZE, scalar2=None, op0=ALU.mult)
+        nc.vector.tensor_scalar(out=nsh8[:], in0=sharp_sb, scalar1=-1.0 / GSIZE, scalar2=None, op0=ALU.mult)
         nc.vector.quantize_mx(out=q_codes[:].bitcast(FP8X4), scales=q_scales[:],
                               in_=q_bf[:].rearrange("p c j -> p (c j)"))
         a_ps = psum.tile([P, SLOTS], F32, name="a_ps")
-        for t in range(PACK):
-            nc.tensor.matmul_mx(out=zh_ps[t][:], lhsT=w_codes[:, t, :].bitcast(FP8X4), lhsT_scale=w_scales[:, t, :],
-                                rhs=tg_words[:].bitcast(FP4X4), rhs_scale=tg_bytes[:], start=True, stop=True)
-            if t == 0:
-                nc.tensor.matmul_mx(out=a_ps[:], lhsT=q_codes[:].bitcast(FP8X4), lhsT_scale=q_scales[:],
-                                    rhs=kg_words[:].bitcast(FP4X4), rhs_scale=kg_bytes[:], start=True, stop=True)
-            nc.scalar.activation(out=ez[t][:], in_=zh_ps[t][:], func=ACT.Exp)
+        nc.tensor.matmul_mx(out=a_ps[:], lhsT=q_codes[:].bitcast(FP8X4), lhsT_scale=q_scales[:],
+                            rhs=kg_words[:].bitcast(FP4X4), rhs_scale=kg_bytes[:], start=True, stop=True)
+        g_raw = tile([P, PACK, ROWS], F32, "g_raw", tag="w_raw0")
+        nc.sync.dma_start(out=g_raw[:], in_=gout.rearrange("(p j) c -> p j c", j=PACK))
+        old_sb = [tile([P, T // 2], F32, "old%d" % h, tag=("lam_sb", "k_bytes")[h]) for h in range(2)]
+        for h in range(2):
+            nc.sync.dma_start(out=old_sb[h][:], in_=old[:, h * T // 2:(h + 1) * T // 2])
 
         a_max = tile([P, GROUPS], F32, "a_max")
-        nc.vector.tensor_reduce(out=a_max[:], in_=by_group(a_ps[:]), axis=AX.X, op=ALU.max)
-
         a_sum = tile([P, GROUPS], F32, "a_sum")
         a_rel = tile([P, SLOTS], F32, "a_rel")
         neg_ms = tile([P, GROUPS], F32, "neg_ms")
         neg_top = tile([P, 1], F32, "neg_top")
+        nc.vector.tensor_reduce(out=a_max[:], in_=by_group(a_ps[:]), axis=AX.X, op=ALU.max)
         nc.vector.tensor_reduce(out=a_sum[:], in_=by_group(a_ps[:]), axis=AX.X, op=ALU.add)
         nc.vector.tensor_tensor(out=by_group(a_rel[:]), in0=by_group(a_ps[:]), in1=over_group(a_max[:]), op=ALU.subtract)
         nc.vector.tensor_scalar(out=neg_ms[:], in0=a_sum[:], scalar1=nsh8[:], scalar2=None,
                                 op0=ALU.mult, op1=ALU.min, accum_out=neg_top[:])
-        p = tile([P, SLOTS], F32, "p")
-        pg = tile([P, GROUPS], F32, "pg")
-        z = tile([P, 1], F32, "z")
-        nc.scalar.activation(out=p[:], in_=a_rel[:], func=ACT.Exp)
-        nc.scalar.activation(out=pg[:], in_=neg_ms[:], func=ACT.Exp, scale=-1.0, bias=neg_top[:], accum_out=z[:])
 
-        s = tile([P, GROUPS], F32, "s")
-        rs = tile([P, GROUPS], F32, "rs")
-        rz = tile([P, 1], F32, "rz")
-        w512 = tile([P, GROUPS], F32, "w512")
-        nws = tile([P, GROUPS], F32, "nws")
-        pn = tile([P, SLOTS], F32, "pn")
-        weight = tile([P, SLOTS], F32, "weight")
-        nc.vector.tensor_reduce(out=s[:], in_=by_group(p[:]), axis=AX.X, op=ALU.add)
-        nc.vector.reciprocal(out=rz[:], in_=z[:])
-        nc.vector.reciprocal(out=rs[:], in_=s[:])
-        nc.vector.tensor_scalar(out=w512[:], in0=pg[:], scalar1=rz[:], scalar2=512.0, op0=ALU.mult, op1=ALU.mult)
-        nc.vector.tensor_tensor(out=by_group(pn[:]), in0=by_group(p[:]), in1=over_group(rs[:]), op=ALU.mult)
-        nc.vector.tensor_scalar(out=nws[:], in0=pg[:], scalar1=rz[:], scalar2=nsh8[:], op0=ALU.mult, op1=ALU.mult)
-        nc.vector.tensor_tensor(out=by_group(weight[:]), in0=by_group(pn[:]), in1=over_group(w512[:]), op=ALU.mult)
-
+        one = tile([P, 1], F32, "one", tag="zero")
+        nc.gpsimd.memset(one[:], 1.0)
         own = tile([P, PACK, SLOTS], F32, "own")
         linked = tile([P, PACK, SLOTS], F32, "linked")
         for t in range(PACK):
-            nc.scalar.activation(out=ht[t][:, 0:SLOTS], in_=ez[t][:], func=ACT.Ln, bias=1.0)
+            nc.scalar.activation(out=ht[t][:, 0:SLOTS], in_=ez[t][:], func=ACT.Ln, bias=one[:])
         for t in range(PACK):
             nc.vector.tensor_tensor(linked[:, t, :], ht[t][:].indirect(idx3[:]), lh[t][:], ALU.mult)
             nc.scalar.activation(out=own[:, t, :], in_=ht[t][:, 0:SLOTS], func=ACT.Copy, scale=hsc_sb[:, t:t + 1])
@@ -189,9 +168,14 @@ def tile_attend_blrlent_bygroup_kernel(tc, query, keys_words, keys_scales, sharp
         g_bf = tile([P, ROWS, PACK], BF16, "g_bf")
         g_codes = tile([P, ROWS], U32, "g_codes")
         g_scales = tile([P, ROWS], U8, "g_scales")
-        interleave(g_bf, g_raw)
-        spread = tile([P, SLOTS], F32, "spread")
-        nc.scalar.activation(out=spread[:], in_=pn[:], func=ACT.Identity, scale=-1.0, bias=sh8[:])
+        interleave(nc.scalar.copy, g_bf, g_raw[:])
+
+        exps = tile([P, SLOTS + GROUPS + 8], F32, "exps", tag="hsc_sb")
+        p = exps[:, 0:SLOTS]
+        pg = exps[:, SLOTS:SLOTS + GROUPS]
+        z = exps[:, SLOTS + GROUPS:SLOTS + GROUPS + 1]
+        nc.scalar.activation(out=p, in_=a_rel[:], func=ACT.Exp)
+        nc.scalar.activation(out=pg, in_=neg_ms[:], func=ACT.Exp, scale=-1.0, bias=neg_top[:], accum_out=z)
 
         h_bf = [tile([P, HALF, PACK], BF16, "h_bf%d" % h) for h in range(2)]
         h_codes = [tile([P, HALF], U32, "h_codes%d" % h) for h in range(2)]
@@ -201,32 +185,65 @@ def tile_attend_blrlent_bygroup_kernel(tc, query, keys_words, keys_scales, sharp
             nc.vector.tensor_tensor(out=h_bf[h][:].rearrange("p (c i) t -> p c t i", i=4),
                                     in0=own[:, :, cols].rearrange("p t (c i) -> p c t i", i=4),
                                     in1=linked[:, :, cols].rearrange("p t (c i) -> p c t i", i=4), op=ALU.add)
-        nc.vector.quantize_mx(out=g_codes[:].bitcast(FP8X4), scales=g_scales[:],
-                              in_=g_bf[:].rearrange("p c j -> p (c j)"))
-        c0_ps = psum.tile([P, SLOTS], F32, name="c0_ps")
-        for h in range(2):
+
+        s = tile([P, GROUPS], F32, "s", tag="own")
+        rs = tile([P, GROUPS], F32, "rs")
+        rz = tile([P, 1], F32, "rz")
+        w512 = tile([P, GROUPS], F32, "w512")
+        nws = tile([P, GROUPS], F32, "nws")
+        share = tile([P, GROUPS], F32, "share")
+        c0_ps = [psum.tile([P, HALF], F32, name="c0_%d" % h) for h in range(2)]
+
+        def read_half(h):
             nc.vector.quantize_mx(out=h_codes[h][:].bitcast(FP8X4), scales=h_scales[h][:],
                                   in_=h_bf[h][:].rearrange("p c t -> p (c t)"))
-            nc.tensor.matmul_mx(out=c0_ps[:, h * HALF:(h + 1) * HALF], lhsT=g_codes[:].bitcast(FP8X4),
+            nc.tensor.matmul_mx(out=c0_ps[h][:], lhsT=g_codes[:].bitcast(FP8X4),
                                 lhsT_scale=g_scales[:], rhs=h_codes[h][:].bitcast(FP8X4), rhs_scale=h_scales[h][:],
                                 start=True, stop=True)
 
+        nc.vector.tensor_reduce(out=s[:], in_=by_group(p), axis=AX.X, op=ALU.add)
+        nc.vector.quantize_mx(out=g_codes[:].bitcast(FP8X4), scales=g_scales[:],
+                              in_=g_bf[:].rearrange("p c j -> p (c j)"))
+        nc.vector.reciprocal(out=rz[:], in_=z)
+        read_half(0)
+        nc.vector.reciprocal(out=rs[:], in_=s[:])
+        nc.vector.tensor_scalar(out=w512[:], in0=pg, scalar1=rz[:], scalar2=512.0, op0=ALU.mult, op1=ALU.mult)
+        read_half(1)
+        nc.vector.tensor_tensor(out=share[:], in0=w512[:], in1=rs[:], op=ALU.mult)
+        nc.vector.tensor_scalar(out=nws[:], in0=pg, scalar1=rz[:], scalar2=nsh8[:], op0=ALU.mult, op1=ALU.mult)
+
+        weight = tile([P, SLOTS], F32, "weight")
         direct = tile([P, SLOTS], F32, "direct")
-        total = tile([P, 1], F32, "total")
+        total = [tile([P, 1], F32, "total%d" % h) for h in range(2)]
         v = tile([P, GROUPS], F32, "v")
+        part_centre = tile([P, GROUPS], F32, "part_centre")
+        slots = [slice(h * HALF, (h + 1) * HALF) for h in range(2)]
+        groups = [slice(h * GROUPS // 2, (h + 1) * GROUPS // 2) for h in range(2)]
+        for h in range(2):
+            nc.vector.tensor_tensor(out=by_group(weight[:, slots[h]]), in0=by_group(p[:, slots[h]]),
+                                    in1=over_group(share[:, groups[h]]), op=ALU.mult)
+        for h in range(2):
+            nc.vector.scalar_tensor_tensor(out=direct[:, slots[h]], in0=c0_ps[h][:], scalar=1.0, in1=weight[:, slots[h]],
+                                           op0=ALU.mult, op1=ALU.mult, accum_out=total[h][:])
+        centre = tile([P, GROUPS], F32, "centre")
+        back = tile([P, GROUPS], F32, "back")
+        e1 = tile([P, GROUPS], F32, "e1")
         first = tile([P, SLOTS], F32, "first")
         second = tile([P, SLOTS], F32, "second")
-        nc.vector.scalar_tensor_tensor(out=direct[:], in0=c0_ps[:], scalar=1.0, in1=weight[:],
-                                       op0=ALU.mult, op1=ALU.mult, accum_out=total[:])
-        nc.vector.tensor_reduce(out=v[:], in_=by_group(direct[:]), axis=AX.X, op=ALU.add)
-        nc.vector.scalar_tensor_tensor(out=by_group(first[:]), in0=over_group(nws[:]), scalar=total[:],
-                                       in1=by_group(direct[:]), op0=ALU.mult, op1=ALU.add)
-        nc.vector.tensor_tensor(out=by_group(second[:]), in0=by_group(spread[:]), in1=over_group(v[:]), op=ALU.mult)
+        nc.vector.tensor_reduce(out=v[:, groups[0]], in_=by_group(direct[:, slots[0]]), axis=AX.X, op=ALU.add)
+        nc.vector.tensor_scalar(out=part_centre[:], in0=nws[:], scalar1=total[0][:], scalar2=None, op0=ALU.mult)
+        nc.vector.tensor_reduce(out=v[:, groups[1]], in_=by_group(direct[:, slots[1]]), axis=AX.X, op=ALU.add)
+        nc.vector.scalar_tensor_tensor(out=centre[:], in0=nws[:], scalar=total[1][:], in1=part_centre[:],
+                                       op0=ALU.mult, op1=ALU.add)
+        nc.vector.scalar_tensor_tensor(out=back[:], in0=v[:], scalar=-1.0, in1=rs[:], op0=ALU.mult, op1=ALU.mult)
+        nc.vector.scalar_tensor_tensor(out=e1[:], in0=v[:], scalar=sh8[:], in1=centre[:], op0=ALU.mult, op1=ALU.add)
+        nc.vector.tensor_tensor(out=by_group(second[:]), in0=by_group(p), in1=over_group(back[:]), op=ALU.mult)
+        nc.vector.tensor_tensor(out=by_group(first[:]), in0=by_group(direct[:]), in1=over_group(e1[:]), op=ALU.add)
         nc.vector.tensor_tensor(placed[:].indirect(idx[:]), first[:], second[:], ALU.add)
 
-        for c in range(T // CHUNK):
-            cols = slice(c * CHUNK, (c + 1) * CHUNK)
-            part = old_sb[c // 2][:, (c % 2) * CHUNK:(c % 2 + 1) * CHUNK]
+        for c, (c0, c1) in enumerate(((0, 512), (512, 1024), (1024, 1536), (1536, 1792), (1792, 2048))):
+            cols = slice(c0, c1)
+            part = old_sb[c0 // 1024][:, c0 % 1024:c0 % 1024 + c1 - c0]
             nc.vector.tensor_tensor(out=part, in0=part, in1=placed[:, cols], op=ALU.add)
             queue = nc.sync if c % 2 == 0 else nc.scalar
             queue.dma_start(out=out[:, cols], in_=part)

@@ -20,13 +20,18 @@ T = 2048
 SLOTS = 512
 ROWS = 128
 HIDDEN = 512
+FEATURES = 512
 GROUPS = 64
 GSIZE = 8
+GAIN = 512.0
+PER_COLUMN = 16
 WINDOW = SLOTS + 32
 HALF = SLOTS // 2
-CHUNK = 512
+RUN = 4
+SCALAR_SHARE = 48
+EDGES = (0, 256, 768, 1280, 1792, T)
 
-FLOPS = 2 * 512 * 128 * 512 * 2 + 2 * 512 * 512 * 512
+FLOPS = 2 * FEATURES * SLOTS * (ROWS + HIDDEN + ROWS)
 
 
 def over_group(ap):
@@ -48,13 +53,14 @@ def tile_attend_blrlent_bygroup_kernel(tc, query, keys_words, keys_scales, sharp
         def tile(shape, dtype, name, tag=None):
             return sb.tile(shape, dtype, name=name, tag=tag or name, align_bytes=64)
 
-        idx = lists.tile([P, SLOTS // 16], U16, name="idx")
-        idx3 = lists.tile([P, SLOTS // 16], U16, name="idx3")
+        idx = lists.tile([P, SLOTS // PER_COLUMN], U16, name="idx")
+        idx3 = lists.tile([P, SLOTS // PER_COLUMN], U16, name="idx3")
 
         k_bytes = tile([P, T], U8, "k_bytes")
         t_words = tile([P, T], U16, "t_words")
         t_bytes = tile([P, T], U8, "t_bytes")
-        w_raw = [tile([P, PACK, HIDDEN // 2], F32, "w_raw%d" % h) for h in range(2)]
+        w_raw = tile([P, PACK, HIDDEN], F32, "w_raw")
+        q_raw = tile([P, PACK, ROWS], F32, "q_raw")
         lam_sb = tile([P, PACK], F32, "lam_sb")
         hsc_sb = tile([P, PACK], F32, "hsc_sb")
         placed = tile([P, T], F32, "placed")
@@ -66,21 +72,20 @@ def tile_attend_blrlent_bygroup_kernel(tc, query, keys_words, keys_scales, sharp
             nc.gpsimd.memset(ht[t][:, SLOTS:WINDOW], 0.0)
         nc.vector.memset(placed[:], 0.0)
 
-        def load_bytes(queues, dst, src):
-            for quad, queue in enumerate(queues):
+        def load_bytes(queue, dst, src):
+            for quad in range(4):
                 queue.dma_start(out=dst[32 * quad:32 * quad + 4, :].bitcast(I32),
                                 in_=src[0, 4 * quad:4 * quad + 4, :].bitcast(I32))
 
-        w_view = w1.rearrange("(p j) c -> p j c", j=PACK)
         nc.sync.dma_start(idx[:], offs)
         nc.sync.dma_start(out=lam_sb[:], in_=lam.rearrange("(p t) o -> p (t o)", t=PACK))
         nc.sync.dma_start(out=hsc_sb[:], in_=hsc.rearrange("(p t) o -> p (t o)", t=PACK))
-        nc.sync.dma_start(idx3[:], offs3)
         nc.sync.dma_start(out=t_words[:].bitcast(I32), in_=tab_words[0].bitcast(I32))
-        load_bytes([nc.scalar] * 4, t_bytes, tab_scales)
-        nc.sync.dma_start(out=w_raw[0][:], in_=w_view[:, :, 0:HIDDEN // 2])
-        nc.sync.dma_start(out=w_raw[1][:], in_=w_view[:, :, HIDDEN // 2:HIDDEN])
-        load_bytes([nc.sync, nc.gpsimd, nc.gpsimd, nc.gpsimd], k_bytes, keys_scales)
+        load_bytes(nc.scalar, t_bytes, tab_scales)
+        nc.sync.dma_start(out=w_raw[:], in_=w1.rearrange("(p j) c -> p j c", j=PACK))
+        nc.sync.dma_start(out=q_raw[:], in_=query.rearrange("(p j) c -> p j c", j=PACK))
+        nc.sync.dma_start(idx3[:], offs3)
+        load_bytes(nc.sync, k_bytes, keys_scales)
 
         lh = [tile([P, SLOTS], F32, "lh%d" % t) for t in range(PACK)]
         for t in range(PACK):
@@ -94,22 +99,22 @@ def tile_attend_blrlent_bygroup_kernel(tc, query, keys_words, keys_scales, sharp
         tg_bytes = tile([P, SLOTS], U8, "tg_bytes")
         nc.vector.tensor_copy(tg_words[:], t_words[:].indirect(idx[:]))
         nc.vector.tensor_copy(tg_bytes[:], t_bytes[:].indirect(idx[:]))
-        q_and_sharp = tile([P, PACK * ROWS + 8], F32, "q_and_sharp", tag="t_words")
-        q_raw = q_and_sharp[:, 0:PACK * ROWS].rearrange("p (j c) -> p j c", j=PACK)
-        sharp_sb = q_and_sharp[:, PACK * ROWS:PACK * ROWS + 1]
-        nc.sync.dma_start(out=q_raw, in_=query.rearrange("(p j) c -> p j c", j=PACK))
-        nc.sync.dma_start(out=sharp_sb, in_=sharp)
+        sharp_sb = tile([P, 1], F32, "sharp_sb", tag="t_words")
+        nc.sync.dma_start(out=sharp_sb[:], in_=sharp)
 
-        def interleave(copy, dst, src):
-            copy(out=dst[:].rearrange("p (c i) j -> p c j i", i=4), in_=src.rearrange("p j (c i) -> p c j i", i=4))
+        def interleave(dst, src):
+            nc.scalar.copy(out=dst[:].rearrange("p (c i) j -> p c j i", i=RUN),
+                           in_=src[:].rearrange("p j (c i) -> p c j i", i=RUN))
 
         w_bf = tile([P, PACK, P, PACK], BF16, "w_bf")
-        for copy, h, m0, m1 in ((nc.scalar.copy, 0, 0, 64), (nc.scalar.copy, 1, 0, 24), (nc.vector.tensor_copy, 1, 24, 64)):
-            copy(out=w_bf[:, :, 64 * h + m0:64 * h + m1, :].rearrange("p t m j -> p m j t"),
-                 in_=w_raw[h][:, :, PACK * m0:PACK * m1].rearrange("p j (m t) -> p m j t", t=PACK))
+        for copy, m0, m1 in ((nc.scalar.copy, 0, SCALAR_SHARE), (nc.vector.tensor_copy, SCALAR_SHARE, P)):
+            copy(out=w_bf[:, :, m0:m1, :].rearrange("p t m j -> p m j t"),
+                 in_=w_raw[:, :, PACK * m0:PACK * m1].rearrange("p j (m t) -> p m j t", t=PACK))
+        q_bf = tile([P, ROWS, PACK], BF16, "q_bf")
+        interleave(q_bf, q_raw)
 
-        zero = tile([P, 1], F32, "zero")
-        nc.gpsimd.memset(zero[:], 0.0)
+        act_bias = tile([P, 1], F32, "act_bias")
+        nc.gpsimd.memset(act_bias[:], 0.0)
         w_codes = [tile([P, P], U32, "w_codes%d" % t) for t in range(PACK)]
         w_scales = [tile([P, P], U8, "w_scales%d" % t) for t in range(PACK)]
         zh_ps = [psum.tile([P, SLOTS], F32, name="zh%d" % t) for t in range(PACK)]
@@ -119,48 +124,52 @@ def tile_attend_blrlent_bygroup_kernel(tc, query, keys_words, keys_scales, sharp
                                   in_=w_bf[:, t, :, :].rearrange("p m j -> p (m j)"))
             nc.tensor.matmul_mx(out=zh_ps[t][:], lhsT=w_codes[t][:].bitcast(FP8X4), lhsT_scale=w_scales[t][:],
                                 rhs=tg_words[:].bitcast(FP4X4), rhs_scale=tg_bytes[:], start=True, stop=True)
-            nc.scalar.activation(out=ez[t][:], in_=zh_ps[t][:], func=ACT.Exp, bias=zero[:])
+            nc.scalar.activation(out=ez[t][:], in_=zh_ps[t][:], func=ACT.Exp, bias=act_bias[:])
 
-        kg_words = tile([P, SLOTS], U16, "kg_words", tag="w_bf")
-        kg_bytes = tile([P, SLOTS], U8, "kg_bytes", tag="w_scales0")
-        nc.vector.tensor_copy(kg_words[:], k_words[:].indirect(idx[:]))
-        nc.vector.tensor_copy(kg_bytes[:], k_bytes[:].indirect(idx[:]))
-        q_bf = tile([P, ROWS, PACK], BF16, "q_bf", tag="w_codes0")
-        q_codes = tile([P, ROWS], U32, "q_codes")
+        slots = [slice(h * HALF, (h + 1) * HALF) for h in range(2)]
+        groups = [slice(h * GROUPS // 2, (h + 1) * GROUPS // 2) for h in range(2)]
+        q_codes = tile([P, ROWS], U32, "q_codes", tag="w_codes0")
         q_scales = tile([P, ROWS], U8, "q_scales")
-        interleave(nc.vector.tensor_copy, q_bf, q_raw)
-        sh8 = tile([P, 1], F32, "sh8")
-        nsh8 = tile([P, 1], F32, "nsh8")
-        nc.vector.tensor_scalar(out=sh8[:], in0=sharp_sb, scalar1=1.0 / GSIZE, scalar2=None, op0=ALU.mult)
-        nc.vector.tensor_scalar(out=nsh8[:], in0=sharp_sb, scalar1=-1.0 / GSIZE, scalar2=None, op0=ALU.mult)
+        kg_words = tile([P, SLOTS], U16, "kg_words", tag="w_scales0")
+        kg_bytes = tile([P, SLOTS], U8, "kg_bytes", tag="w_bf")
+        nc.vector.tensor_copy(kg_bytes[:], k_bytes[:].indirect(idx[:]))
         nc.vector.quantize_mx(out=q_codes[:].bitcast(FP8X4), scales=q_scales[:],
                               in_=q_bf[:].rearrange("p c j -> p (c j)"))
-        a_ps = psum.tile([P, SLOTS], F32, name="a_ps")
-        nc.tensor.matmul_mx(out=a_ps[:], lhsT=q_codes[:].bitcast(FP8X4), lhsT_scale=q_scales[:],
-                            rhs=kg_words[:].bitcast(FP4X4), rhs_scale=kg_bytes[:], start=True, stop=True)
-        g_raw = tile([P, PACK, ROWS], F32, "g_raw", tag="w_raw0")
-        nc.sync.dma_start(out=g_raw[:], in_=gout.rearrange("(p j) c -> p j c", j=PACK))
-        old_sb = [tile([P, T // 2], F32, "old%d" % h, tag=("lam_sb", "k_bytes")[h]) for h in range(2)]
+        a_ps = [psum.tile([P, HALF], F32, name="a_%d" % h) for h in range(2)]
         for h in range(2):
-            nc.sync.dma_start(out=old_sb[h][:], in_=old[:, h * T // 2:(h + 1) * T // 2])
+            entries = idx[:, h * HALF // PER_COLUMN:(h + 1) * HALF // PER_COLUMN]
+            nc.vector.tensor_copy(kg_words[:, slots[h]], k_words[:].indirect(entries))
+            nc.tensor.matmul_mx(out=a_ps[h][:], lhsT=q_codes[:].bitcast(FP8X4), lhsT_scale=q_scales[:],
+                                rhs=kg_words[:, slots[h]].bitcast(FP4X4), rhs_scale=kg_bytes[:, slots[h]],
+                                start=True, stop=True)
+        sh8 = tile([P, 1], F32, "sh8")
+        nsh8 = tile([P, 1], F32, "nsh8")
+        nc.vector.tensor_scalar(out=sh8[:], in0=sharp_sb[:], scalar1=1.0 / GSIZE, scalar2=None, op0=ALU.mult)
+        nc.vector.tensor_scalar(out=nsh8[:], in0=sharp_sb[:], scalar1=-1.0 / GSIZE, scalar2=None, op0=ALU.mult)
+        g_raw = tile([P, PACK, ROWS], F32, "g_raw", tag="q_raw")
+        nc.sync.dma_start(out=g_raw[:], in_=gout.rearrange("(p j) c -> p j c", j=PACK))
+        old_sb = tile([P, T], F32, "old_sb", tag="lam_sb")
+        nc.sync.dma_start(out=old_sb[:], in_=old)
 
         a_max = tile([P, GROUPS], F32, "a_max")
         a_sum = tile([P, GROUPS], F32, "a_sum")
         a_rel = tile([P, SLOTS], F32, "a_rel")
         neg_ms = tile([P, GROUPS], F32, "neg_ms")
         neg_top = tile([P, 1], F32, "neg_top")
-        nc.vector.tensor_reduce(out=a_max[:], in_=by_group(a_ps[:]), axis=AX.X, op=ALU.max)
-        nc.vector.tensor_reduce(out=a_sum[:], in_=by_group(a_ps[:]), axis=AX.X, op=ALU.add)
-        nc.vector.tensor_tensor(out=by_group(a_rel[:]), in0=by_group(a_ps[:]), in1=over_group(a_max[:]), op=ALU.subtract)
+        for h in range(2):
+            nc.vector.tensor_reduce(out=a_max[:, groups[h]], in_=by_group(a_ps[h][:]), axis=AX.X, op=ALU.max)
+            nc.vector.tensor_reduce(out=a_sum[:, groups[h]], in_=by_group(a_ps[h][:]), axis=AX.X, op=ALU.add)
+        for h in range(2):
+            nc.vector.tensor_tensor(out=by_group(a_rel[:, slots[h]]), in0=by_group(a_ps[h][:]),
+                                    in1=over_group(a_max[:, groups[h]]), op=ALU.subtract)
         nc.vector.tensor_scalar(out=neg_ms[:], in0=a_sum[:], scalar1=nsh8[:], scalar2=None,
                                 op0=ALU.mult, op1=ALU.min, accum_out=neg_top[:])
 
-        one = tile([P, 1], F32, "one", tag="zero")
-        nc.gpsimd.memset(one[:], 1.0)
+        nc.scalar.activation(out=act_bias[:], in_=act_bias[:], func=ACT.Identity, bias=1.0)
         own = tile([P, PACK, SLOTS], F32, "own")
         linked = tile([P, PACK, SLOTS], F32, "linked")
         for t in range(PACK):
-            nc.scalar.activation(out=ht[t][:, 0:SLOTS], in_=ez[t][:], func=ACT.Ln, bias=one[:])
+            nc.scalar.activation(out=ht[t][:, 0:SLOTS], in_=ez[t][:], func=ACT.Ln, bias=act_bias[:])
         for t in range(PACK):
             nc.vector.tensor_tensor(linked[:, t, :], ht[t][:].indirect(idx3[:]), lh[t][:], ALU.mult)
             nc.scalar.activation(out=own[:, t, :], in_=ht[t][:, 0:SLOTS], func=ACT.Copy, scale=hsc_sb[:, t:t + 1])
@@ -168,9 +177,9 @@ def tile_attend_blrlent_bygroup_kernel(tc, query, keys_words, keys_scales, sharp
         g_bf = tile([P, ROWS, PACK], BF16, "g_bf")
         g_codes = tile([P, ROWS], U32, "g_codes")
         g_scales = tile([P, ROWS], U8, "g_scales")
-        interleave(nc.scalar.copy, g_bf, g_raw[:])
+        interleave(g_bf, g_raw)
 
-        exps = tile([P, SLOTS + GROUPS + 8], F32, "exps", tag="hsc_sb")
+        exps = tile([P, SLOTS + GROUPS + GSIZE], F32, "exps", tag="hsc_sb")
         p = exps[:, 0:SLOTS]
         pg = exps[:, SLOTS:SLOTS + GROUPS]
         z = exps[:, SLOTS + GROUPS:SLOTS + GROUPS + 1]
@@ -181,15 +190,13 @@ def tile_attend_blrlent_bygroup_kernel(tc, query, keys_words, keys_scales, sharp
         h_codes = [tile([P, HALF], U32, "h_codes%d" % h) for h in range(2)]
         h_scales = [tile([P, HALF], U8, "h_scales%d" % h) for h in range(2)]
         for h in range(2):
-            cols = slice(h * HALF, (h + 1) * HALF)
-            nc.vector.tensor_tensor(out=h_bf[h][:].rearrange("p (c i) t -> p c t i", i=4),
-                                    in0=own[:, :, cols].rearrange("p t (c i) -> p c t i", i=4),
-                                    in1=linked[:, :, cols].rearrange("p t (c i) -> p c t i", i=4), op=ALU.add)
+            nc.vector.tensor_tensor(out=h_bf[h][:].rearrange("p (c i) t -> p c t i", i=RUN),
+                                    in0=own[:, :, slots[h]].rearrange("p t (c i) -> p c t i", i=RUN),
+                                    in1=linked[:, :, slots[h]].rearrange("p t (c i) -> p c t i", i=RUN), op=ALU.add)
 
         s = tile([P, GROUPS], F32, "s", tag="own")
         rs = tile([P, GROUPS], F32, "rs")
         rz = tile([P, 1], F32, "rz")
-        w512 = tile([P, GROUPS], F32, "w512")
         nws = tile([P, GROUPS], F32, "nws")
         share = tile([P, GROUPS], F32, "share")
         c0_ps = [psum.tile([P, HALF], F32, name="c0_%d" % h) for h in range(2)]
@@ -207,9 +214,8 @@ def tile_attend_blrlent_bygroup_kernel(tc, query, keys_words, keys_scales, sharp
         nc.vector.reciprocal(out=rz[:], in_=z)
         read_half(0)
         nc.vector.reciprocal(out=rs[:], in_=s[:])
-        nc.vector.tensor_scalar(out=w512[:], in0=pg, scalar1=rz[:], scalar2=512.0, op0=ALU.mult, op1=ALU.mult)
         read_half(1)
-        nc.vector.tensor_tensor(out=share[:], in0=w512[:], in1=rs[:], op=ALU.mult)
+        nc.vector.scalar_tensor_tensor(out=share[:], in0=pg, scalar=rz[:], in1=rs[:], op0=ALU.mult, op1=ALU.mult)
         nc.vector.tensor_scalar(out=nws[:], in0=pg, scalar1=rz[:], scalar2=nsh8[:], op0=ALU.mult, op1=ALU.mult)
 
         weight = tile([P, SLOTS], F32, "weight")
@@ -217,13 +223,11 @@ def tile_attend_blrlent_bygroup_kernel(tc, query, keys_words, keys_scales, sharp
         total = [tile([P, 1], F32, "total%d" % h) for h in range(2)]
         v = tile([P, GROUPS], F32, "v")
         part_centre = tile([P, GROUPS], F32, "part_centre")
-        slots = [slice(h * HALF, (h + 1) * HALF) for h in range(2)]
-        groups = [slice(h * GROUPS // 2, (h + 1) * GROUPS // 2) for h in range(2)]
         for h in range(2):
             nc.vector.tensor_tensor(out=by_group(weight[:, slots[h]]), in0=by_group(p[:, slots[h]]),
                                     in1=over_group(share[:, groups[h]]), op=ALU.mult)
         for h in range(2):
-            nc.vector.scalar_tensor_tensor(out=direct[:, slots[h]], in0=c0_ps[h][:], scalar=1.0, in1=weight[:, slots[h]],
+            nc.vector.scalar_tensor_tensor(out=direct[:, slots[h]], in0=c0_ps[h][:], scalar=GAIN, in1=weight[:, slots[h]],
                                            op0=ALU.mult, op1=ALU.mult, accum_out=total[h][:])
         centre = tile([P, GROUPS], F32, "centre")
         back = tile([P, GROUPS], F32, "back")
@@ -241,9 +245,8 @@ def tile_attend_blrlent_bygroup_kernel(tc, query, keys_words, keys_scales, sharp
         nc.vector.tensor_tensor(out=by_group(first[:]), in0=by_group(direct[:]), in1=over_group(e1[:]), op=ALU.add)
         nc.vector.tensor_tensor(placed[:].indirect(idx[:]), first[:], second[:], ALU.add)
 
-        for c, (c0, c1) in enumerate(((0, 512), (512, 1024), (1024, 1536), (1536, 1792), (1792, 2048))):
-            cols = slice(c0, c1)
-            part = old_sb[c0 // 1024][:, c0 % 1024:c0 % 1024 + c1 - c0]
-            nc.vector.tensor_tensor(out=part, in0=part, in1=placed[:, cols], op=ALU.add)
-            queue = nc.sync if c % 2 == 0 else nc.scalar
-            queue.dma_start(out=out[:, cols], in_=part)
+        for piece in range(len(EDGES) - 1):
+            cols = slice(EDGES[piece], EDGES[piece + 1])
+            nc.vector.tensor_tensor(out=old_sb[:, cols], in0=old_sb[:, cols], in1=placed[:, cols], op=ALU.add)
+            queue = nc.sync if piece % 2 == 0 else nc.scalar
+            queue.dma_start(out=out[:, cols], in_=old_sb[:, cols])

from contextlib import ExitStack

import concourse.mybir as mybir

F32 = mybir.dt.float32
BF16 = mybir.dt.bfloat16
I32 = mybir.dt.int32
U32 = mybir.dt.uint32
U16 = mybir.dt.uint16
U8 = mybir.dt.uint8
FP8X4 = mybir.dt.float8_e4m3fn_x4
FP4X4 = mybir.dt.float4_e2m1fn_x4
ALU = mybir.AluOpType
ACT = mybir.ActivationFunctionType
AX = mybir.AxisListType

P = 128
PACK = 4
T = 2048
SLOTS = 512
ROWS = 128
HIDDEN = 512
FEATURES = 512
GROUPS = 64
GSIZE = 8
GAIN = 512.0
PER_COLUMN = 16
WINDOW = SLOTS + 32
HALF = SLOTS // 2
RUN = 4
SCALAR_SHARE = 48
EDGES = (0, 256, 768, 1280, 1792, T)

FLOPS = 2 * FEATURES * SLOTS * (ROWS + HIDDEN + ROWS)


def over_group(ap):
    return ap.rearrange("p (g o) -> p g o", o=1).to_broadcast([P, ap.shape[1], GSIZE])


def by_group(ap):
    return ap.rearrange("p (g j) -> p g j", j=GSIZE)


def tile_attend_blrlent_bygroup_kernel(tc, query, keys_words, keys_scales, sharp, tab_words, tab_scales,
                                        w1, lam, gout, hsc, old, offs3, offs, out):
    nc = tc.nc
    with ExitStack() as ctx:
        lists = ctx.enter_context(tc.tile_pool(name="lists", bufs=1))
        sb = ctx.enter_context(tc.tile_pool(name="sb", bufs=1))
        psum = ctx.enter_context(tc.psum_pool(name="psum", bufs=1))

        def tile(shape, dtype, name, tag=None):
            return sb.tile(shape, dtype, name=name, tag=tag or name, align_bytes=64)

        idx = lists.tile([P, SLOTS // PER_COLUMN], U16, name="idx")
        idx3 = lists.tile([P, SLOTS // PER_COLUMN], U16, name="idx3")

        k_bytes = tile([P, T], U8, "k_bytes")
        t_words = tile([P, T], U16, "t_words")
        t_bytes = tile([P, T], U8, "t_bytes")
        w_raw = tile([P, PACK, HIDDEN], F32, "w_raw")
        q_raw = tile([P, PACK, ROWS], F32, "q_raw")
        lam_sb = tile([P, PACK], F32, "lam_sb")
        hsc_sb = tile([P, PACK], F32, "hsc_sb")
        placed = tile([P, T], F32, "placed")
        ht = [tile([P, WINDOW], F32, "ht%d" % t) for t in range(PACK)]

        nc.gpsimd.memset(t_bytes[:].bitcast(I32), 0)
        nc.vector.memset(k_bytes[:].bitcast(I32), 0)
        for t in range(PACK):
            nc.gpsimd.memset(ht[t][:, SLOTS:WINDOW], 0.0)
        nc.vector.memset(placed[:], 0.0)

        def load_bytes(queue, dst, src):
            for quad in range(4):
                queue.dma_start(out=dst[32 * quad:32 * quad + 4, :].bitcast(I32),
                                in_=src[0, 4 * quad:4 * quad + 4, :].bitcast(I32))

        nc.sync.dma_start(idx[:], offs)
        nc.sync.dma_start(out=lam_sb[:], in_=lam.rearrange("(p t) o -> p (t o)", t=PACK))
        nc.sync.dma_start(out=hsc_sb[:], in_=hsc.rearrange("(p t) o -> p (t o)", t=PACK))
        nc.sync.dma_start(out=t_words[:].bitcast(I32), in_=tab_words[0].bitcast(I32))
        load_bytes(nc.scalar, t_bytes, tab_scales)
        nc.sync.dma_start(out=w_raw[:], in_=w1.rearrange("(p j) c -> p j c", j=PACK))
        nc.sync.dma_start(out=q_raw[:], in_=query.rearrange("(p j) c -> p j c", j=PACK))
        nc.sync.dma_start(idx3[:], offs3)
        load_bytes(nc.sync, k_bytes, keys_scales)

        lh = [tile([P, SLOTS], F32, "lh%d" % t) for t in range(PACK)]
        for t in range(PACK):
            nc.vector.tensor_scalar(out=lh[t][:], in0=lam_sb[:, t:t + 1].to_broadcast([P, SLOTS]),
                                    scalar1=hsc_sb[:, t:t + 1], scalar2=None, op0=ALU.mult)

        k_words = tile([P, T], U16, "k_words", tag="lam_sb")
        nc.sync.dma_start(out=k_words[:].bitcast(I32), in_=keys_words[0].bitcast(I32))

        tg_words = tile([P, SLOTS], U16, "tg_words")
        tg_bytes = tile([P, SLOTS], U8, "tg_bytes")
        nc.vector.tensor_copy(tg_words[:], t_words[:].indirect(idx[:]))
        nc.vector.tensor_copy(tg_bytes[:], t_bytes[:].indirect(idx[:]))
        sharp_sb = tile([P, 1], F32, "sharp_sb", tag="t_words")
        nc.sync.dma_start(out=sharp_sb[:], in_=sharp)

        def interleave(dst, src):
            nc.scalar.copy(out=dst[:].rearrange("p (c i) j -> p c j i", i=RUN),
                           in_=src[:].rearrange("p j (c i) -> p c j i", i=RUN))

        w_bf = tile([P, PACK, P, PACK], BF16, "w_bf")
        for copy, m0, m1 in ((nc.scalar.copy, 0, SCALAR_SHARE), (nc.vector.tensor_copy, SCALAR_SHARE, P)):
            copy(out=w_bf[:, :, m0:m1, :].rearrange("p t m j -> p m j t"),
                 in_=w_raw[:, :, PACK * m0:PACK * m1].rearrange("p j (m t) -> p m j t", t=PACK))
        q_bf = tile([P, ROWS, PACK], BF16, "q_bf")
        interleave(q_bf, q_raw)

        act_bias = tile([P, 1], F32, "act_bias")
        nc.gpsimd.memset(act_bias[:], 0.0)
        w_codes = [tile([P, P], U32, "w_codes%d" % t) for t in range(PACK)]
        w_scales = [tile([P, P], U8, "w_scales%d" % t) for t in range(PACK)]
        zh_ps = [psum.tile([P, SLOTS], F32, name="zh%d" % t) for t in range(PACK)]
        ez = [tile([P, SLOTS], F32, "ez%d" % t) for t in range(PACK)]
        for t in range(PACK):
            nc.vector.quantize_mx(out=w_codes[t][:].bitcast(FP8X4), scales=w_scales[t][:],
                                  in_=w_bf[:, t, :, :].rearrange("p m j -> p (m j)"))
            nc.tensor.matmul_mx(out=zh_ps[t][:], lhsT=w_codes[t][:].bitcast(FP8X4), lhsT_scale=w_scales[t][:],
                                rhs=tg_words[:].bitcast(FP4X4), rhs_scale=tg_bytes[:], start=True, stop=True)
            nc.scalar.activation(out=ez[t][:], in_=zh_ps[t][:], func=ACT.Exp, bias=act_bias[:])

        slots = [slice(h * HALF, (h + 1) * HALF) for h in range(2)]
        groups = [slice(h * GROUPS // 2, (h + 1) * GROUPS // 2) for h in range(2)]
        q_codes = tile([P, ROWS], U32, "q_codes", tag="w_codes0")
        q_scales = tile([P, ROWS], U8, "q_scales")
        kg_words = tile([P, SLOTS], U16, "kg_words", tag="w_scales0")
        kg_bytes = tile([P, SLOTS], U8, "kg_bytes", tag="w_bf")
        nc.vector.tensor_copy(kg_bytes[:], k_bytes[:].indirect(idx[:]))
        nc.vector.quantize_mx(out=q_codes[:].bitcast(FP8X4), scales=q_scales[:],
                              in_=q_bf[:].rearrange("p c j -> p (c j)"))
        a_ps = [psum.tile([P, HALF], F32, name="a_%d" % h) for h in range(2)]
        for h in range(2):
            entries = idx[:, h * HALF // PER_COLUMN:(h + 1) * HALF // PER_COLUMN]
            nc.vector.tensor_copy(kg_words[:, slots[h]], k_words[:].indirect(entries))
            nc.tensor.matmul_mx(out=a_ps[h][:], lhsT=q_codes[:].bitcast(FP8X4), lhsT_scale=q_scales[:],
                                rhs=kg_words[:, slots[h]].bitcast(FP4X4), rhs_scale=kg_bytes[:, slots[h]],
                                start=True, stop=True)
        sh8 = tile([P, 1], F32, "sh8")
        nsh8 = tile([P, 1], F32, "nsh8")
        nc.vector.tensor_scalar(out=sh8[:], in0=sharp_sb[:], scalar1=1.0 / GSIZE, scalar2=None, op0=ALU.mult)
        nc.vector.tensor_scalar(out=nsh8[:], in0=sharp_sb[:], scalar1=-1.0 / GSIZE, scalar2=None, op0=ALU.mult)
        g_raw = tile([P, PACK, ROWS], F32, "g_raw", tag="q_raw")
        nc.sync.dma_start(out=g_raw[:], in_=gout.rearrange("(p j) c -> p j c", j=PACK))
        old_sb = tile([P, T], F32, "old_sb", tag="lam_sb")
        nc.sync.dma_start(out=old_sb[:], in_=old)

        a_max = tile([P, GROUPS], F32, "a_max")
        a_sum = tile([P, GROUPS], F32, "a_sum")
        a_rel = tile([P, SLOTS], F32, "a_rel")
        neg_ms = tile([P, GROUPS], F32, "neg_ms")
        neg_top = tile([P, 1], F32, "neg_top")
        for h in range(2):
            nc.vector.tensor_reduce(out=a_max[:, groups[h]], in_=by_group(a_ps[h][:]), axis=AX.X, op=ALU.max)
            nc.vector.tensor_reduce(out=a_sum[:, groups[h]], in_=by_group(a_ps[h][:]), axis=AX.X, op=ALU.add)
        for h in range(2):
            nc.vector.tensor_tensor(out=by_group(a_rel[:, slots[h]]), in0=by_group(a_ps[h][:]),
                                    in1=over_group(a_max[:, groups[h]]), op=ALU.subtract)
        nc.vector.tensor_scalar(out=neg_ms[:], in0=a_sum[:], scalar1=nsh8[:], scalar2=None,
                                op0=ALU.mult, op1=ALU.min, accum_out=neg_top[:])

        nc.scalar.activation(out=act_bias[:], in_=act_bias[:], func=ACT.Identity, bias=1.0)
        own = tile([P, PACK, SLOTS], F32, "own")
        linked = tile([P, PACK, SLOTS], F32, "linked")
        for t in range(PACK):
            nc.scalar.activation(out=ht[t][:, 0:SLOTS], in_=ez[t][:], func=ACT.Ln, bias=act_bias[:])
        for t in range(PACK):
            nc.vector.tensor_tensor(linked[:, t, :], ht[t][:].indirect(idx3[:]), lh[t][:], ALU.mult)
            nc.scalar.activation(out=own[:, t, :], in_=ht[t][:, 0:SLOTS], func=ACT.Copy, scale=hsc_sb[:, t:t + 1])

        g_bf = tile([P, ROWS, PACK], BF16, "g_bf")
        g_codes = tile([P, ROWS], U32, "g_codes")
        g_scales = tile([P, ROWS], U8, "g_scales")
        interleave(g_bf, g_raw)

        exps = tile([P, SLOTS + GROUPS + GSIZE], F32, "exps", tag="hsc_sb")
        p = exps[:, 0:SLOTS]
        pg = exps[:, SLOTS:SLOTS + GROUPS]
        z = exps[:, SLOTS + GROUPS:SLOTS + GROUPS + 1]
        nc.scalar.activation(out=p, in_=a_rel[:], func=ACT.Exp)
        nc.scalar.activation(out=pg, in_=neg_ms[:], func=ACT.Exp, scale=-1.0, bias=neg_top[:], accum_out=z)

        h_bf = [tile([P, HALF, PACK], BF16, "h_bf%d" % h) for h in range(2)]
        h_codes = [tile([P, HALF], U32, "h_codes%d" % h) for h in range(2)]
        h_scales = [tile([P, HALF], U8, "h_scales%d" % h) for h in range(2)]
        for h in range(2):
            nc.vector.tensor_tensor(out=h_bf[h][:].rearrange("p (c i) t -> p c t i", i=RUN),
                                    in0=own[:, :, slots[h]].rearrange("p t (c i) -> p c t i", i=RUN),
                                    in1=linked[:, :, slots[h]].rearrange("p t (c i) -> p c t i", i=RUN), op=ALU.add)

        s = tile([P, GROUPS], F32, "s", tag="own")
        rs = tile([P, GROUPS], F32, "rs")
        rz = tile([P, 1], F32, "rz")
        nws = tile([P, GROUPS], F32, "nws")
        share = tile([P, GROUPS], F32, "share")
        c0_ps = [psum.tile([P, HALF], F32, name="c0_%d" % h) for h in range(2)]

        def read_half(h):
            nc.vector.quantize_mx(out=h_codes[h][:].bitcast(FP8X4), scales=h_scales[h][:],
                                  in_=h_bf[h][:].rearrange("p c t -> p (c t)"))
            nc.tensor.matmul_mx(out=c0_ps[h][:], lhsT=g_codes[:].bitcast(FP8X4),
                                lhsT_scale=g_scales[:], rhs=h_codes[h][:].bitcast(FP8X4), rhs_scale=h_scales[h][:],
                                start=True, stop=True)

        nc.vector.tensor_reduce(out=s[:], in_=by_group(p), axis=AX.X, op=ALU.add)
        nc.vector.quantize_mx(out=g_codes[:].bitcast(FP8X4), scales=g_scales[:],
                              in_=g_bf[:].rearrange("p c j -> p (c j)"))
        nc.vector.reciprocal(out=rz[:], in_=z)
        read_half(0)
        nc.vector.reciprocal(out=rs[:], in_=s[:])
        read_half(1)
        nc.vector.scalar_tensor_tensor(out=share[:], in0=pg, scalar=rz[:], in1=rs[:], op0=ALU.mult, op1=ALU.mult)
        nc.vector.tensor_scalar(out=nws[:], in0=pg, scalar1=rz[:], scalar2=nsh8[:], op0=ALU.mult, op1=ALU.mult)

        weight = tile([P, SLOTS], F32, "weight")
        direct = tile([P, SLOTS], F32, "direct")
        total = [tile([P, 1], F32, "total%d" % h) for h in range(2)]
        v = tile([P, GROUPS], F32, "v")
        part_centre = tile([P, GROUPS], F32, "part_centre")
        for h in range(2):
            nc.vector.tensor_tensor(out=by_group(weight[:, slots[h]]), in0=by_group(p[:, slots[h]]),
                                    in1=over_group(share[:, groups[h]]), op=ALU.mult)
        for h in range(2):
            nc.vector.scalar_tensor_tensor(out=direct[:, slots[h]], in0=c0_ps[h][:], scalar=GAIN, in1=weight[:, slots[h]],
                                           op0=ALU.mult, op1=ALU.mult, accum_out=total[h][:])
        centre = tile([P, GROUPS], F32, "centre")
        back = tile([P, GROUPS], F32, "back")
        e1 = tile([P, GROUPS], F32, "e1")
        first = tile([P, SLOTS], F32, "first")
        second = tile([P, SLOTS], F32, "second")
        nc.vector.tensor_reduce(out=v[:, groups[0]], in_=by_group(direct[:, slots[0]]), axis=AX.X, op=ALU.add)
        nc.vector.tensor_scalar(out=part_centre[:], in0=nws[:], scalar1=total[0][:], scalar2=None, op0=ALU.mult)
        nc.vector.tensor_reduce(out=v[:, groups[1]], in_=by_group(direct[:, slots[1]]), axis=AX.X, op=ALU.add)
        nc.vector.scalar_tensor_tensor(out=centre[:], in0=nws[:], scalar=total[1][:], in1=part_centre[:],
                                       op0=ALU.mult, op1=ALU.add)
        nc.vector.scalar_tensor_tensor(out=back[:], in0=v[:], scalar=-1.0, in1=rs[:], op0=ALU.mult, op1=ALU.mult)
        nc.vector.scalar_tensor_tensor(out=e1[:], in0=v[:], scalar=sh8[:], in1=centre[:], op0=ALU.mult, op1=ALU.add)
        nc.vector.tensor_tensor(out=by_group(second[:]), in0=by_group(p), in1=over_group(back[:]), op=ALU.mult)
        nc.vector.tensor_tensor(out=by_group(first[:]), in0=by_group(direct[:]), in1=over_group(e1[:]), op=ALU.add)
        nc.vector.tensor_tensor(placed[:].indirect(idx[:]), first[:], second[:], ALU.add)

        for piece in range(len(EDGES) - 1):
            cols = slice(EDGES[piece], EDGES[piece + 1])
            nc.vector.tensor_tensor(out=old_sb[:, cols], in0=old_sb[:, cols], in1=placed[:, cols], op=ALU.add)
            queue = nc.sync if piece % 2 == 0 else nc.scalar
            queue.dma_start(out=out[:, cols], in_=old_sb[:, cols])
